import numpy as np
import ml_dtypes


def mxq(x, axis, fmt="e4m3"):
    dtype, down = {"e4m3": (ml_dtypes.float8_e4m3fn, 7), "e5m2": (ml_dtypes.float8_e5m2, 14)}[fmt]
    v = np.moveaxis(np.asarray(x, np.float32).astype(ml_dtypes.bfloat16).astype(np.float64), axis, -1)
    blocks = v.reshape(v.shape[:-1] + (-1, 32))
    amax = np.abs(blocks).max(-1, keepdims=True)
    byte = np.maximum(np.where(amax > 0, np.frexp(amax)[1] - 1 + 127, 0) - down, 1)
    scale = np.exp2(byte - 127.0)
    codes = (blocks / scale).astype(np.float32).astype(dtype).astype(np.float64)
    return np.moveaxis((codes * scale).reshape(v.shape), -1, axis)


WIDE = False


def mx_kscale(k):
    if not WIDE:
        return np.ones(k)
    levels = np.array([10, -10, 5, -5, 0])
    if k % 512:
        return np.exp2(np.random.permutation(np.resize(levels, k // 32))).repeat(32)
    a = np.empty((k // 512, 16))
    for p in range(k // 512):
        a[p, :8] = np.random.permutation(np.resize(levels, 8))
        for g in range(8):
            far = levels[np.abs(levels - a[p, g]) >= 10]
            a[p, g + 8] = far[np.random.randint(len(far))]
    return np.exp2(a.ravel()).repeat(32)


def f64(x):
    return np.asarray(x).astype(np.float64)


def striped(idx):
    return np.tile(idx.reshape(-1, 16).T, (8, 1)).astype(np.uint16)


def unstriped(offs):
    return offs[:16].T.reshape(-1).astype(np.int64)


K, T, S, N = 1024, 2048, 1024, 256
P = 2 ** 7


def setup_inputs():
    n = np.random.standard_normal
    s = mx_kscale(K)[:, None]
    return {
        "xT": (n((K, T)) * s).astype(np.float32),
        "mean": np.tile(0.3 * np.random.standard_normal(T), (P, 1)).astype(np.float32),
        "inv": np.tile(np.random.uniform(0.5, 2.0, T), (P, 1)).astype(np.float32),
        "gsum": n((N, 1)).astype(np.float32),
        "b": (0.3 * n((N, 1))).astype(np.float32),
        "w1": (n((K, N)) / np.sqrt(K) / s).astype(np.float32),
        "offs": striped(np.random.permutation(T)[:S]),
    }


def reference(xT, mean, inv, gsum, b, w1, offs):
    xq = mxq(f64(xT)[:, unstriped(offs)], 0, "e4m3")
    y = mxq(f64(w1), 0, "e4m3").T @ xq
    mg = f64(mean)[:1][:, unstriped(offs)]
    ig = f64(inv)[:1][:, unstriped(offs)]
    return (y - (f64(gsum) * mg)) * ig + f64(b)

@@ -1,0 +1,195 @@
+from contextlib import ExitStack
+
+import concourse.mybir as mybir
+from concourse.masks import make_identity
+
+K, T, S, N = 1024, 2048, 1024, 256
+FLOPS = 2 * K * S * N
+BYTES = 4 * (K * T + K * N + N * S + 2 * T + 2 * N) + 2 * 128 * (S // 16)
+
+F32 = mybir.dt.float32
+BF16 = mybir.dt.bfloat16
+U32 = mybir.dt.uint32
+I32 = mybir.dt.int32
+U16 = mybir.dt.uint16
+U8 = mybir.dt.uint8
+FP8X4 = mybir.dt.float8_e4m3fn_x4
+MULT = mybir.AluOpType.mult
+ADD = mybir.AluOpType.add
+COPY = mybir.ActivationFunctionType.Copy
+
+P = 128
+PACK = 4
+K_PASS = P * PACK
+BANK = 512
+CHUNK = 256
+CHUNKS = S // CHUNK
+TILES = S // P
+EARLY = 6
+LOADS = [[1024, 1024], [1024, 1024], [1024, 512, 512], [1024, 512, 256, 256]]
+ON_VECTOR = [(1, 1), (2, 2), (3, 1), (3, 3)]
+
+
+def tile_picked_lnfold_none_l_kernel(tc, xT, mean, inv, gsum, b, w1, offs, out):
+    nc = tc.nc
+    with ExitStack() as ctx:
+        keep = ctx.enter_context(tc.tile_pool(name="keep", bufs=1))
+        psum_y = ctx.enter_context(tc.psum_pool(name="psum_y", bufs=EARLY))
+        psum_o = ctx.enter_context(tc.psum_pool(name="psum_o", bufs=2))
+
+        offsets = keep.tile([P, S // 16], U16, name="offsets")
+        nc.sync.dma_start(offsets[:], offs)
+
+        stats = keep.tile([P, T], F32, name="stats")
+        nc.sync.dma_start(stats[P - 2 : P - 1, :], mean[0:1, :])
+        nc.sync.dma_start(stats[P - 1 : P, :], inv[0:1, :])
+        nc.vector.memset(stats[0 : P - 2, :], 0.0)
+        g_col = keep.tile([P, 2], F32, name="g_col")
+        b_col = keep.tile([P, 2], F32, name="b_col")
+        nc.scalar.dma_start(g_col[:], gsum.rearrange("(p t) o -> p (t o)", p=P))
+        nc.scalar.dma_start(b_col[:], b.rearrange("(p t) o -> p (t o)", p=P))
+
+        x_rows = xT.rearrange("(g p u e) t -> g u p e t", p=P, u=2, e=2)
+        raw = {}
+
+        def load_pair(q):
+            c0 = 0
+            for i, width in enumerate(LOADS[q]):
+                piece = keep.tile([P, 2, width], F32, name="raw%d_%d" % (q, i))
+                nc.sync.dma_start(piece[:], x_rows[q // 2, q % 2][:, :, c0 : c0 + width])
+                raw[q, i] = piece
+                c0 = c0 + width
+
+        load_pair(0)
+        load_pair(1)
+        w_raw = keep.tile([P, 2, PACK, N], F32, name="w_raw")
+        nc.sync.dma_start(w_raw[:], w1.rearrange("(g p j) n -> p g j n", p=P, j=PACK))
+        load_pair(2)
+        load_pair(3)
+
+        neg_g = keep.tile([P, 2], F32, name="neg_g")
+        nc.scalar.mul(neg_g[:], g_col[:], -1.0)
+        ident = keep.tile([P, P], F32, name="ident")
+        make_identity(nc, ident[:])
+
+        picked = keep.tile([P, S], F32, name="picked")
+        nc.vector.tensor_copy(picked[:], stats[:].indirect(offsets[:]))
+        tok = keep.tile([P, TILES, 2], F32, name="tok")
+        for h in range(2):
+            bank = psum_o.tile([P, 4, P], F32, name="o_bank", tag="o")
+            for i in range(4):
+                t = 4 * h + i
+                nc.tensor.transpose(bank[:, i, :], picked[:, t * P : (t + 1) * P], ident[:])
+            nc.vector.tensor_copy(tok[:, 4 * h : 4 * h + 4, :], bank[:, :, P - 2 : P])
+        shift = keep.tile([P, TILES], F32, name="shift")
+        nc.vector.tensor_tensor(shift[:], tok[:, :, 0], tok[:, :, 1], MULT)
+        offset_term = keep.tile([P, CHUNKS, 2, CHUNK], F32, name="offset_term")
+        for h in range(2):
+            bank = psum_o.tile([P, 2, CHUNK], F32, name="o_bank", tag="o")
+            flat = bank[:].rearrange("p c j -> p (c j)")
+            for i in range(4):
+                t = 4 * h + i
+                nc.tensor.transpose(flat[:, i * P : (i + 1) * P], shift[:, t : t + 1].to_broadcast([P, P]), ident[:])
+            for m in range(2):
+                nc.vector.tensor_scalar(offset_term[:, 2 * h : 2 * h + 2, m, :], bank[:], neg_g[:, m : m + 1], b_col[:, m : m + 1], MULT, ADD)
+
+        pairs = [keep.tile([P, T, 2], BF16, name="pairs%d" % q, align_bytes=64) for q in range(4)]
+        words = [keep.tile([P, 2, S], U32, name="words%d" % g, align_bytes=64) for g in range(2)]
+
+        def cast_pair(q):
+            c0 = 0
+            for i, width in enumerate(LOADS[q]):
+                src = raw[q, i][:].rearrange("p e t -> p t e")
+                dst = pairs[q][:, c0 : c0 + width, :]
+                if (q, i) in ON_VECTOR:
+                    nc.vector.tensor_copy(dst, src)
+                else:
+                    nc.scalar.copy(dst, src)
+                c0 = c0 + width
+
+        def gather(q, j0, j1):
+            window = pairs[q][:].rearrange("p t e -> p (t e)").bitcast(U32)
+            nc.vector.tensor_copy(words[q // 2][:, q % 2, j0:j1], window.indirect(offsets[:, j0 // 16 : j1 // 16]))
+
+        cast_pair(0)
+        gather(0, 0, S)
+        cast_pair(1)
+        gather(1, 0, S)
+        x0 = keep.tile([P, S * PACK], BF16, name="x0", align_bytes=64)
+        nc.vector.tensor_copy(x0[:].bitcast(I32).rearrange("p (j u) -> p j u", u=2), words[0][:].bitcast(I32).rearrange("p u j -> p j u"))
+        w_bf = keep.tile([P, 2, N, PACK], BF16, name="w_bf", align_bytes=64)
+        for g in range(2):
+            nc.scalar.copy(w_bf[:, g].rearrange("p (m r) j -> p m r j", m=2), w_raw[:, g].rearrange("p j (r m) -> p m r j", m=2))
+        x0_codes = keep.tile([P, S], U32, name="x0_codes", align_bytes=64)
+        x0_scales = keep.tile([P, S], U8, name="x0_scales", align_bytes=64)
+        nc.vector.quantize_mx(out=x0_codes[:].bitcast(FP8X4), scales=x0_scales[:], in_=x0[:])
+        w_codes = keep.tile([P, 2 * N], U32, name="w_codes", align_bytes=64)
+        w_scales = keep.tile([P, 2 * N], U8, name="w_scales", align_bytes=64)
+        nc.vector.quantize_mx(out=w_codes[:].bitcast(FP8X4), scales=w_scales[:], in_=w_bf[:].rearrange("p g n j -> p (g n j)"))
+
+        def product(acc, codes, scales, c0, g):
+            nc.tensor.matmul_mx(
+                out=acc[:, 0:N],
+                lhsT=codes[:, c0 : c0 + P].bitcast(FP8X4),
+                lhsT_scale=scales[:, c0 : c0 + P],
+                rhs=w_codes[:, g * N : (g + 1) * N].bitcast(FP8X4),
+                rhs_scale=w_scales[:, g * N : (g + 1) * N],
+                start=(g == 0),
+                stop=(g == 1),
+            )
+
+        sums = {}
+        for t in range(EARLY):
+            sums[t] = psum_y.tile([P, BANK], F32, name="y_bank", tag="y")
+            product(sums[t], x0_codes, x0_scales, t * P, 0)
+
+        cast_pair(2)
+        gather(2, 0, S)
+        cast_pair(3)
+
+        x1, x1_codes, x1_scales, scaled, turned = {}, {}, {}, {}, {}
+        out_rows = out.rearrange("(p m) j -> p m j", p=P)
+
+        def weave(c):
+            x1[c] = keep.tile([P, CHUNK * PACK], BF16, name="x1_%d" % c, align_bytes=64)
+            nc.scalar.copy(x1[c][:].bitcast(U32).rearrange("p (j u) -> p j u", u=2), words[1][:, :, c * CHUNK : (c + 1) * CHUNK].rearrange("p u j -> p j u"))
+
+        def quantise(c):
+            x1_codes[c] = keep.tile([P, CHUNK], U32, name="x1_codes%d" % c, align_bytes=64)
+            x1_scales[c] = keep.tile([P, CHUNK], U8, name="x1_scales%d" % c, align_bytes=64)
+            nc.vector.quantize_mx(out=x1_codes[c][:].bitcast(FP8X4), scales=x1_scales[c][:], in_=x1[c][:])
+
+        def multiply(c):
+            for h in range(2):
+                t = 2 * c + h
+                if t >= EARLY:
+                    sums[t] = psum_y.tile([P, BANK], F32, name="y_bank", tag="y")
+                    product(sums[t], x0_codes, x0_scales, t * P, 0)
+                product(sums[t], x1_codes[c], x1_scales[c], h * P, 1)
+            for h in range(2):
+                t = 2 * c + h
+                scaled[t] = keep.tile([P, N], F32, name="scaled%d" % t)
+                nc.scalar.activation(scaled[t][:], sums[t][:, 0:N], COPY, scale=tok[:, t, 1:2])
+
+        def turn(c):
+            turned[c] = psum_o.tile([P, 2, CHUNK], F32, name="o_bank", tag="o")
+            for h in range(2):
+                for m in range(2):
+                    nc.tensor.transpose(turned[c][:, m, h * P : (h + 1) * P], scaled[2 * c + h][:, m * P : (m + 1) * P], ident[:])
+
+        def finish(c):
+            result = keep.tile([P, 2, CHUNK], F32, name="result%d" % c)
+            nc.vector.tensor_tensor(result[:], turned[c][:], offset_term[:, c], ADD)
+            nc.sync.dma_start(out_rows[:, :, c * CHUNK : (c + 1) * CHUNK], result[:])
+
+        for step in range(CHUNKS + 3):
+            if step < CHUNKS:
+                gather(3, step * CHUNK, (step + 1) * CHUNK)
+                weave(step)
+            if 0 <= step - 1 < CHUNKS:
+                quantise(step - 1)
+                multiply(step - 1)
+            if 0 <= step - 2 < CHUNKS:
+                turn(step - 2)
+            if 0 <= step - 3 < CHUNKS:
+                finish(step - 3)

@@ -14,182 +14,169 @@ I32 = mybir.dt.int32
 U16 = mybir.dt.uint16
 U8 = mybir.dt.uint8
 FP8X4 = mybir.dt.float8_e4m3fn_x4
-MULT = mybir.AluOpType.mult
 ADD = mybir.AluOpType.add
+IDENTITY = mybir.ActivationFunctionType.Identity
 COPY = mybir.ActivationFunctionType.Copy
 
 P = 128
 PACK = 4
-K_PASS = P * PACK
 BANK = 512
 CHUNK = 256
 CHUNKS = S // CHUNK
 TILES = S // P
-EARLY = 6
-LOADS = [[1024, 1024], [1024, 1024], [1024, 512, 512], [1024, 512, 256, 256]]
-ON_VECTOR = [(1, 1), (2, 2), (3, 1), (3, 3)]
+LOADS = [[1024, 1024], [1024, 1024], [1024, 1024], [1024, 512, 256, 256]]
+VECTOR_COLUMNS = [[1024, 1024], [768, 640], [0, 512], [0, 512, 256, 256]]
 
 
 def tile_picked_lnfold_none_l_kernel(tc, xT, mean, inv, gsum, b, w1, offs, out):
     nc = tc.nc
     with ExitStack() as ctx:
         keep = ctx.enter_context(tc.tile_pool(name="keep", bufs=1))
-        psum_y = ctx.enter_context(tc.psum_pool(name="psum_y", bufs=EARLY))
-        psum_o = ctx.enter_context(tc.psum_pool(name="psum_o", bufs=2))
+        psum = ctx.enter_context(tc.psum_pool(name="psum", bufs=TILES))
 
         offsets = keep.tile([P, S // 16], U16, name="offsets")
         nc.sync.dma_start(offsets[:], offs)
-
         stats = keep.tile([P, T], F32, name="stats")
         nc.sync.dma_start(stats[P - 2 : P - 1, :], mean[0:1, :])
         nc.sync.dma_start(stats[P - 1 : P, :], inv[0:1, :])
-        nc.vector.memset(stats[0 : P - 2, :], 0.0)
-        g_col = keep.tile([P, 2], F32, name="g_col")
-        b_col = keep.tile([P, 2], F32, name="b_col")
-        nc.scalar.dma_start(g_col[:], gsum.rearrange("(p t) o -> p (t o)", p=P))
-        nc.scalar.dma_start(b_col[:], b.rearrange("(p t) o -> p (t o)", p=P))
+        nc.vector.memset(stats[0 : P - 2, :].bitcast(I32), 0)
 
         x_rows = xT.rearrange("(g p u e) t -> g u p e t", p=P, u=2, e=2)
         raw = {}
 
-        def load_pair(q):
-            c0 = 0
-            for i, width in enumerate(LOADS[q]):
-                piece = keep.tile([P, 2, width], F32, name="raw%d_%d" % (q, i))
-                nc.sync.dma_start(piece[:], x_rows[q // 2, q % 2][:, :, c0 : c0 + width])
-                raw[q, i] = piece
-                c0 = c0 + width
+        def load_piece(q, i):
+            c0 = sum(LOADS[q][:i])
+            raw[q, i] = keep.tile([P, 2, LOADS[q][i]], F32, name="raw%d_%d" % (q, i), align_bytes=64)
+            nc.sync.dma_start(raw[q, i][:], x_rows[q // 2, q % 2][:, :, c0 : c0 + LOADS[q][i]])
 
-        load_pair(0)
+        def load_pair(q):
+            for i in range(len(LOADS[q])):
+                load_piece(q, i)
+
+        load_piece(0, 0)
+        channel_rows = keep.tile([P, P], F32, name="channel_rows")
+        nc.sync.dma_start(channel_rows[P - 4 : P - 2, :], gsum.rearrange("(m r) o -> m (r o)", m=2))
+        nc.sync.dma_start(channel_rows[P - 2 : P, :], b.rearrange("(m r) o -> m (r o)", m=2))
+        nc.gpsimd.memset(channel_rows[0 : P - 4, :], 0.0)
+        load_piece(0, 1)
         load_pair(1)
+        load_pair(2)
         w_raw = keep.tile([P, 2, PACK, N], F32, name="w_raw")
         nc.sync.dma_start(w_raw[:], w1.rearrange("(g p j) n -> p g j n", p=P, j=PACK))
-        load_pair(2)
         load_pair(3)
 
-        neg_g = keep.tile([P, 2], F32, name="neg_g")
-        nc.scalar.mul(neg_g[:], g_col[:], -1.0)
         ident = keep.tile([P, P], F32, name="ident")
         make_identity(nc, ident[:])
 
-        picked = keep.tile([P, S], F32, name="picked")
-        nc.vector.tensor_copy(picked[:], stats[:].indirect(offsets[:]))
-        tok = keep.tile([P, TILES, 2], F32, name="tok")
-        for h in range(2):
-            bank = psum_o.tile([P, 4, P], F32, name="o_bank", tag="o")
-            for i in range(4):
-                t = 4 * h + i
-                nc.tensor.transpose(bank[:, i, :], picked[:, t * P : (t + 1) * P], ident[:])
-            nc.vector.tensor_copy(tok[:, 4 * h : 4 * h + 4, :], bank[:, :, P - 2 : P])
-        shift = keep.tile([P, TILES], F32, name="shift")
-        nc.vector.tensor_tensor(shift[:], tok[:, :, 0], tok[:, :, 1], MULT)
-        offset_term = keep.tile([P, CHUNKS, 2, CHUNK], F32, name="offset_term")
-        for h in range(2):
-            bank = psum_o.tile([P, 2, CHUNK], F32, name="o_bank", tag="o")
-            flat = bank[:].rearrange("p c j -> p (c j)")
-            for i in range(4):
-                t = 4 * h + i
-                nc.tensor.transpose(flat[:, i * P : (i + 1) * P], shift[:, t : t + 1].to_broadcast([P, P]), ident[:])
-            for m in range(2):
-                nc.vector.tensor_scalar(offset_term[:, 2 * h : 2 * h + 2, m, :], bank[:], neg_g[:, m : m + 1], b_col[:, m : m + 1], MULT, ADD)
-
         pairs = [keep.tile([P, T, 2], BF16, name="pairs%d" % q, align_bytes=64) for q in range(4)]
-        words = [keep.tile([P, 2, S], U32, name="words%d" % g, align_bytes=64) for g in range(2)]
 
         def cast_pair(q):
             c0 = 0
             for i, width in enumerate(LOADS[q]):
                 src = raw[q, i][:].rearrange("p e t -> p t e")
                 dst = pairs[q][:, c0 : c0 + width, :]
-                if (q, i) in ON_VECTOR:
-                    nc.vector.tensor_copy(dst, src)
-                else:
-                    nc.scalar.copy(dst, src)
+                cut = width - VECTOR_COLUMNS[q][i]
+                if cut > 0:
+                    nc.scalar.copy(dst[:, 0:cut, :], src[:, 0:cut, :])
+                if cut < width:
+                    nc.vector.tensor_copy(dst[:, cut:width, :], src[:, cut:width, :])
                 c0 = c0 + width
 
-        def gather(q, j0, j1):
+        def gather(dst, q, j0, j1):
             window = pairs[q][:].rearrange("p t e -> p (t e)").bitcast(U32)
-            nc.vector.tensor_copy(words[q // 2][:, q % 2, j0:j1], window.indirect(offsets[:, j0 // 16 : j1 // 16]))
+            nc.vector.tensor_copy(dst, window.indirect(offsets[:, j0 // 16 : j1 // 16]))
 
+        channel = keep.tile([P, 4], F32, name="channel")
+        bank = psum.tile([P, 4, P], F32, name="bank", tag="bank")
+        nc.tensor.transpose(bank[:, 0, :], channel_rows[:], ident[:])
+        nc.scalar.mul(channel[:, 0:2], bank[:, 0, P - 4 : P - 2], -1.0)
+        nc.scalar.copy(channel[:, 2:4], bank[:, 0, P - 2 : P])
+        tok = keep.tile([P, TILES, 2], F32, name="tok")
+        shift = keep.tile([P, TILES], F32, name="shift")
+        offset_term = keep.tile([P, CHUNKS, 2, CHUNK], F32, name="offset_term")
+        for h in range(2):
+            picked = keep.tile([P, BANK], F32, name="picked%d" % h)
+            nc.vector.tensor_copy(picked[:], stats[:].indirect(offsets[:, h * BANK // 16 : (h + 1) * BANK // 16]))
+            bank = psum.tile([P, 4, P], F32, name="bank", tag="bank")
+            for i in range(4):
+                nc.tensor.transpose(bank[:, i, :], picked[:, i * P : (i + 1) * P], ident[:])
+            nc.scalar.copy(tok[:, 4 * h : 4 * h + 4, :], bank[:, :, P - 2 : P])
+            for t in range(4 * h, 4 * h + 4):
+                nc.scalar.activation(shift[:, t : t + 1], tok[:, t, 0:1], COPY, scale=tok[:, t, 1:2])
+            bank = psum.tile([P, 2, CHUNK], F32, name="bank", tag="bank")
+            flat = bank[:].rearrange("p c j -> p (c j)")
+            for i in range(4):
+                t = 4 * h + i
+                nc.tensor.transpose(flat[:, i * P : (i + 1) * P], shift[:, t : t + 1].to_broadcast([P, P]), ident[:])
+            for m in range(2):
+                nc.scalar.activation(offset_term[:, 2 * h : 2 * h + 2, m, :], bank[:], IDENTITY, bias=channel[:, 2 + m : 3 + m], scale=channel[:, m : m + 1])
+
+        words0 = keep.tile([P, 2, S], U32, name="words0", align_bytes=64)
         cast_pair(0)
-        gather(0, 0, S)
+        gather(words0[:, 0, :], 0, 0, S)
         cast_pair(1)
-        gather(1, 0, S)
+        gather(words0[:, 1, :], 1, 0, S)
         x0 = keep.tile([P, S * PACK], BF16, name="x0", align_bytes=64)
-        nc.vector.tensor_copy(x0[:].bitcast(I32).rearrange("p (j u) -> p j u", u=2), words[0][:].bitcast(I32).rearrange("p u j -> p j u"))
+        nc.vector.tensor_copy(x0[:].bitcast(I32).rearrange("p (j u) -> p j u", u=2), words0[:].bitcast(I32).rearrange("p u j -> p j u"))
+        words1 = keep.tile([P, 2, S], U32, name="words1", align_bytes=64)
+        cast_pair(2)
+        gather(words1[:, 0, :], 2, 0, S)
         w_bf = keep.tile([P, 2, N, PACK], BF16, name="w_bf", align_bytes=64)
         for g in range(2):
-            nc.scalar.copy(w_bf[:, g].rearrange("p (m r) j -> p m r j", m=2), w_raw[:, g].rearrange("p j (r m) -> p m r j", m=2))
+            nc.scalar.copy(w_bf[:, g].rearrange("p (c i) j -> p c j i", i=PACK), w_raw[:, g].rearrange("p j (c i) -> p c j i", i=PACK))
         x0_codes = keep.tile([P, S], U32, name="x0_codes", align_bytes=64)
         x0_scales = keep.tile([P, S], U8, name="x0_scales", align_bytes=64)
         nc.vector.quantize_mx(out=x0_codes[:].bitcast(FP8X4), scales=x0_scales[:], in_=x0[:])
-        w_codes = keep.tile([P, 2 * N], U32, name="w_codes", align_bytes=64)
-        w_scales = keep.tile([P, 2 * N], U8, name="w_scales", align_bytes=64)
-        nc.vector.quantize_mx(out=w_codes[:].bitcast(FP8X4), scales=w_scales[:], in_=w_bf[:].rearrange("p g n j -> p (g n j)"))
+        w_codes, w_scales = {}, {}
 
-        def product(acc, codes, scales, c0, g):
+        def quantise_weights(g, tag):
+            w_codes[g] = keep.tile([P, N], U32, name="w_codes%d" % g, tag=tag, align_bytes=64)
+            w_scales[g] = keep.tile([P, N], U8, name="w_scales%d" % g, align_bytes=64)
+            nc.vector.quantize_mx(out=w_codes[g][:].bitcast(FP8X4), scales=w_scales[g][:], in_=w_bf[:, g].rearrange("p n j -> p (n j)"))
+
+        quantise_weights(1, "w_codes1")
+        cast_pair(3)
+        quantise_weights(0, "raw3_2")
+
+        def by_token(acc, codes, scales, c0, g):
             nc.tensor.matmul_mx(
                 out=acc[:, 0:N],
                 lhsT=codes[:, c0 : c0 + P].bitcast(FP8X4),
                 lhsT_scale=scales[:, c0 : c0 + P],
-                rhs=w_codes[:, g * N : (g + 1) * N].bitcast(FP8X4),
-                rhs_scale=w_scales[:, g * N : (g + 1) * N],
+                rhs=w_codes[g][:].bitcast(FP8X4),
+                rhs_scale=w_scales[g][:],
                 start=(g == 0),
                 stop=(g == 1),
             )
 
         sums = {}
-        for t in range(EARLY):
-            sums[t] = psum_y.tile([P, BANK], F32, name="y_bank", tag="y")
-            product(sums[t], x0_codes, x0_scales, t * P, 0)
+        for t in range(TILES):
+            sums[t] = psum.tile([P, BANK], F32, name="bank", tag="bank")
+            by_token(sums[t], x0_codes, x0_scales, t * P, 0)
 
-        cast_pair(2)
-        gather(2, 0, S)
-        cast_pair(3)
-
-        x1, x1_codes, x1_scales, scaled, turned = {}, {}, {}, {}, {}
-        out_rows = out.rearrange("(p m) j -> p m j", p=P)
-
-        def weave(c):
-            x1[c] = keep.tile([P, CHUNK * PACK], BF16, name="x1_%d" % c, align_bytes=64)
-            nc.scalar.copy(x1[c][:].bitcast(U32).rearrange("p (j u) -> p j u", u=2), words[1][:, :, c * CHUNK : (c + 1) * CHUNK].rearrange("p u j -> p j u"))
-
-        def quantise(c):
+        x1_codes, x1_scales = {}, {}
+        out_rows = out.rearrange("(m p) j -> p m j", p=P)
+        for c in range(CHUNKS):
+            cols = slice(c * CHUNK, (c + 1) * CHUNK)
+            gather(words1[:, 1, cols], 3, c * CHUNK, (c + 1) * CHUNK)
+            x1 = keep.tile([P, CHUNK * PACK], BF16, name="x1_%d" % c, align_bytes=64)
+            nc.scalar.copy(x1[:].bitcast(U32).rearrange("p (j u) -> p j u", u=2), words1[:, :, cols].rearrange("p u j -> p j u"))
             x1_codes[c] = keep.tile([P, CHUNK], U32, name="x1_codes%d" % c, align_bytes=64)
             x1_scales[c] = keep.tile([P, CHUNK], U8, name="x1_scales%d" % c, align_bytes=64)
-            nc.vector.quantize_mx(out=x1_codes[c][:].bitcast(FP8X4), scales=x1_scales[c][:], in_=x1[c][:])
-
-        def multiply(c):
+            nc.vector.quantize_mx(out=x1_codes[c][:].bitcast(FP8X4), scales=x1_scales[c][:], in_=x1[:])
             for h in range(2):
-                t = 2 * c + h
-                if t >= EARLY:
-                    sums[t] = psum_y.tile([P, BANK], F32, name="y_bank", tag="y")
-                    product(sums[t], x0_codes, x0_scales, t * P, 0)
-                product(sums[t], x1_codes[c], x1_scales[c], h * P, 1)
-            for h in range(2):
-                t = 2 * c + h
-                scaled[t] = keep.tile([P, N], F32, name="scaled%d" % t)
-                nc.scalar.activation(scaled[t][:], sums[t][:, 0:N], COPY, scale=tok[:, t, 1:2])
+                by_token(sums[2 * c + h], x1_codes[c], x1_scales[c], h * P, 1)
 
-        def turn(c):
-            turned[c] = psum_o.tile([P, 2, CHUNK], F32, name="o_bank", tag="o")
-            for h in range(2):
-                for m in range(2):
-                    nc.tensor.transpose(turned[c][:, m, h * P : (h + 1) * P], scaled[2 * c + h][:, m * P : (m + 1) * P], ident[:])
-
-        def finish(c):
+        for c in range(CHUNKS):
             result = keep.tile([P, 2, CHUNK], F32, name="result%d" % c)
-            nc.vector.tensor_tensor(result[:], turned[c][:], offset_term[:, c], ADD)
-            nc.sync.dma_start(out_rows[:, :, c * CHUNK : (c + 1) * CHUNK], result[:])
-
-        for step in range(CHUNKS + 3):
-            if step < CHUNKS:
-                gather(3, step * CHUNK, (step + 1) * CHUNK)
-                weave(step)
-            if 0 <= step - 1 < CHUNKS:
-                quantise(step - 1)
-                multiply(step - 1)
-            if 0 <= step - 2 < CHUNKS:
-                turn(step - 2)
-            if 0 <= step - 3 < CHUNKS:
-                finish(step - 3)
+            for h in range(2):
+                t, cols = 2 * c + h, slice(h * P, (h + 1) * P)
+                scaled = keep.tile([P, N], F32, name="scaled%d" % t)
+                nc.scalar.activation(scaled[:], sums[t][:, 0:N], COPY, scale=tok[:, t, 1:2])
+                for m in range(2):
+                    nc.tensor.transpose(sums[t][:, N + m * P : N + (m + 1) * P], scaled[:, m * P : (m + 1) * P], ident[:])
+                nc.vector.tensor_tensor(result[:, :, cols], sums[t][:, N:].rearrange("p (m j) -> p m j", m=2), offset_term[:, c, :, cols], ADD)
+                if c == CHUNKS - 1:
+                    nc.sync.dma_start(out_rows[:, :, t * P : (t + 1) * P], result[:, :, cols])
+            if c < CHUNKS - 1:
+                nc.sync.dma_start(out_rows[:, :, c * CHUNK : (c + 1) * CHUNK], result[:])

from contextlib import ExitStack

import concourse.mybir as mybir
from concourse.masks import make_identity

K, T, S, N = 1024, 2048, 1024, 256
FLOPS = 2 * K * S * N
BYTES = 4 * (K * T + K * N + N * S + 2 * T + 2 * N) + 2 * 128 * (S // 16)

F32 = mybir.dt.float32
BF16 = mybir.dt.bfloat16
U32 = mybir.dt.uint32
I32 = mybir.dt.int32
U16 = mybir.dt.uint16
U8 = mybir.dt.uint8
FP8X4 = mybir.dt.float8_e4m3fn_x4
ADD = mybir.AluOpType.add
IDENTITY = mybir.ActivationFunctionType.Identity
COPY = mybir.ActivationFunctionType.Copy

P = 128
PACK = 4
BANK = 512
CHUNK = 256
CHUNKS = S // CHUNK
TILES = S // P
LOADS = [[1024, 1024], [1024, 1024], [1024, 1024], [1024, 512, 256, 256]]
VECTOR_COLUMNS = [[1024, 1024], [768, 640], [0, 512], [0, 512, 256, 256]]


def tile_picked_lnfold_none_l_kernel(tc, xT, mean, inv, gsum, b, w1, offs, out):
    nc = tc.nc
    with ExitStack() as ctx:
        keep = ctx.enter_context(tc.tile_pool(name="keep", bufs=1))
        psum = ctx.enter_context(tc.psum_pool(name="psum", bufs=TILES))

        offsets = keep.tile([P, S // 16], U16, name="offsets")
        nc.sync.dma_start(offsets[:], offs)
        stats = keep.tile([P, T], F32, name="stats")
        nc.sync.dma_start(stats[P - 2 : P - 1, :], mean[0:1, :])
        nc.sync.dma_start(stats[P - 1 : P, :], inv[0:1, :])
        nc.vector.memset(stats[0 : P - 2, :].bitcast(I32), 0)

        x_rows = xT.rearrange("(g p u e) t -> g u p e t", p=P, u=2, e=2)
        raw = {}

        def load_piece(q, i):
            c0 = sum(LOADS[q][:i])
            raw[q, i] = keep.tile([P, 2, LOADS[q][i]], F32, name="raw%d_%d" % (q, i), align_bytes=64)
            nc.sync.dma_start(raw[q, i][:], x_rows[q // 2, q % 2][:, :, c0 : c0 + LOADS[q][i]])

        def load_pair(q):
            for i in range(len(LOADS[q])):
                load_piece(q, i)

        load_piece(0, 0)
        channel_rows = keep.tile([P, P], F32, name="channel_rows")
        nc.sync.dma_start(channel_rows[P - 4 : P - 2, :], gsum.rearrange("(m r) o -> m (r o)", m=2))
        nc.sync.dma_start(channel_rows[P - 2 : P, :], b.rearrange("(m r) o -> m (r o)", m=2))
        nc.gpsimd.memset(channel_rows[0 : P - 4, :], 0.0)
        load_piece(0, 1)
        load_pair(1)
        load_pair(2)
        w_raw = keep.tile([P, 2, PACK, N], F32, name="w_raw")
        nc.sync.dma_start(w_raw[:], w1.rearrange("(g p j) n -> p g j n", p=P, j=PACK))
        load_pair(3)

        ident = keep.tile([P, P], F32, name="ident")
        make_identity(nc, ident[:])

        pairs = [keep.tile([P, T, 2], BF16, name="pairs%d" % q, align_bytes=64) for q in range(4)]

        def cast_pair(q):
            c0 = 0
            for i, width in enumerate(LOADS[q]):
                src = raw[q, i][:].rearrange("p e t -> p t e")
                dst = pairs[q][:, c0 : c0 + width, :]
                cut = width - VECTOR_COLUMNS[q][i]
                if cut > 0:
                    nc.scalar.copy(dst[:, 0:cut, :], src[:, 0:cut, :])
                if cut < width:
                    nc.vector.tensor_copy(dst[:, cut:width, :], src[:, cut:width, :])
                c0 = c0 + width

        def gather(dst, q, j0, j1):
            window = pairs[q][:].rearrange("p t e -> p (t e)").bitcast(U32)
            nc.vector.tensor_copy(dst, window.indirect(offsets[:, j0 // 16 : j1 // 16]))

        channel = keep.tile([P, 4], F32, name="channel")
        bank = psum.tile([P, 4, P], F32, name="bank", tag="bank")
        nc.tensor.transpose(bank[:, 0, :], channel_rows[:], ident[:])
        nc.scalar.mul(channel[:, 0:2], bank[:, 0, P - 4 : P - 2], -1.0)
        nc.scalar.copy(channel[:, 2:4], bank[:, 0, P - 2 : P])
        tok = keep.tile([P, TILES, 2], F32, name="tok")
        shift = keep.tile([P, TILES], F32, name="shift")
        offset_term = keep.tile([P, CHUNKS, 2, CHUNK], F32, name="offset_term")
        for h in range(2):
            picked = keep.tile([P, BANK], F32, name="picked%d" % h)
            nc.vector.tensor_copy(picked[:], stats[:].indirect(offsets[:, h * BANK // 16 : (h + 1) * BANK // 16]))
            bank = psum.tile([P, 4, P], F32, name="bank", tag="bank")
            for i in range(4):
                nc.tensor.transpose(bank[:, i, :], picked[:, i * P : (i + 1) * P], ident[:])
            nc.scalar.copy(tok[:, 4 * h : 4 * h + 4, :], bank[:, :, P - 2 : P])
            for t in range(4 * h, 4 * h + 4):
                nc.scalar.activation(shift[:, t : t + 1], tok[:, t, 0:1], COPY, scale=tok[:, t, 1:2])
            bank = psum.tile([P, 2, CHUNK], F32, name="bank", tag="bank")
            flat = bank[:].rearrange("p c j -> p (c j)")
            for i in range(4):
                t = 4 * h + i
                nc.tensor.transpose(flat[:, i * P : (i + 1) * P], shift[:, t : t + 1].to_broadcast([P, P]), ident[:])
            for m in range(2):
                nc.scalar.activation(offset_term[:, 2 * h : 2 * h + 2, m, :], bank[:], IDENTITY, bias=channel[:, 2 + m : 3 + m], scale=channel[:, m : m + 1])

        words0 = keep.tile([P, 2, S], U32, name="words0", align_bytes=64)
        cast_pair(0)
        gather(words0[:, 0, :], 0, 0, S)
        cast_pair(1)
        gather(words0[:, 1, :], 1, 0, S)
        x0 = keep.tile([P, S * PACK], BF16, name="x0", align_bytes=64)
        nc.vector.tensor_copy(x0[:].bitcast(I32).rearrange("p (j u) -> p j u", u=2), words0[:].bitcast(I32).rearrange("p u j -> p j u"))
        words1 = keep.tile([P, 2, S], U32, name="words1", align_bytes=64)
        cast_pair(2)
        gather(words1[:, 0, :], 2, 0, S)
        w_bf = keep.tile([P, 2, N, PACK], BF16, name="w_bf", align_bytes=64)
        for g in range(2):
            nc.scalar.copy(w_bf[:, g].rearrange("p (c i) j -> p c j i", i=PACK), w_raw[:, g].rearrange("p j (c i) -> p c j i", i=PACK))
        x0_codes = keep.tile([P, S], U32, name="x0_codes", align_bytes=64)
        x0_scales = keep.tile([P, S], U8, name="x0_scales", align_bytes=64)
        nc.vector.quantize_mx(out=x0_codes[:].bitcast(FP8X4), scales=x0_scales[:], in_=x0[:])
        w_codes, w_scales = {}, {}

        def quantise_weights(g, tag):
            w_codes[g] = keep.tile([P, N], U32, name="w_codes%d" % g, tag=tag, align_bytes=64)
            w_scales[g] = keep.tile([P, N], U8, name="w_scales%d" % g, align_bytes=64)
            nc.vector.quantize_mx(out=w_codes[g][:].bitcast(FP8X4), scales=w_scales[g][:], in_=w_bf[:, g].rearrange("p n j -> p (n j)"))

        quantise_weights(1, "w_codes1")
        cast_pair(3)
        quantise_weights(0, "raw3_2")

        def by_token(acc, codes, scales, c0, g):
            nc.tensor.matmul_mx(
                out=acc[:, 0:N],
                lhsT=codes[:, c0 : c0 + P].bitcast(FP8X4),
                lhsT_scale=scales[:, c0 : c0 + P],
                rhs=w_codes[g][:].bitcast(FP8X4),
                rhs_scale=w_scales[g][:],
                start=(g == 0),
                stop=(g == 1),
            )

        sums = {}
        for t in range(TILES):
            sums[t] = psum.tile([P, BANK], F32, name="bank", tag="bank")
            by_token(sums[t], x0_codes, x0_scales, t * P, 0)

        x1_codes, x1_scales = {}, {}
        out_rows = out.rearrange("(m p) j -> p m j", p=P)
        for c in range(CHUNKS):
            cols = slice(c * CHUNK, (c + 1) * CHUNK)
            gather(words1[:, 1, cols], 3, c * CHUNK, (c + 1) * CHUNK)
            x1 = keep.tile([P, CHUNK * PACK], BF16, name="x1_%d" % c, align_bytes=64)
            nc.scalar.copy(x1[:].bitcast(U32).rearrange("p (j u) -> p j u", u=2), words1[:, :, cols].rearrange("p u j -> p j u"))
            x1_codes[c] = keep.tile([P, CHUNK], U32, name="x1_codes%d" % c, align_bytes=64)
            x1_scales[c] = keep.tile([P, CHUNK], U8, name="x1_scales%d" % c, align_bytes=64)
            nc.vector.quantize_mx(out=x1_codes[c][:].bitcast(FP8X4), scales=x1_scales[c][:], in_=x1[:])
            for h in range(2):
                by_token(sums[2 * c + h], x1_codes[c], x1_scales[c], h * P, 1)

        for c in range(CHUNKS):
            result = keep.tile([P, 2, CHUNK], F32, name="result%d" % c)
            for h in range(2):
                t, cols = 2 * c + h, slice(h * P, (h + 1) * P)
                scaled = keep.tile([P, N], F32, name="scaled%d" % t)
                nc.scalar.activation(scaled[:], sums[t][:, 0:N], COPY, scale=tok[:, t, 1:2])
                for m in range(2):
                    nc.tensor.transpose(sums[t][:, N + m * P : N + (m + 1) * P], scaled[:, m * P : (m + 1) * P], ident[:])
                nc.vector.tensor_tensor(result[:, :, cols], sums[t][:, N:].rearrange("p (m j) -> p m j", m=2), offset_term[:, c, :, cols], ADD)
                if c == CHUNKS - 1:
                    nc.sync.dma_start(out_rows[:, :, t * P : (t + 1) * P], result[:, :, cols])
            if c < CHUNKS - 1:
                nc.sync.dma_start(out_rows[:, :, c * CHUNK : (c + 1) * CHUNK], result[:])
